import numpy as np
import ml_dtypes


def mxq(x, axis, fmt="e4m3"):
    dtype, down = {"e4m3": (ml_dtypes.float8_e4m3fn, 7), "e5m2": (ml_dtypes.float8_e5m2, 14)}[fmt]
    v = np.moveaxis(np.asarray(x, np.float32).astype(ml_dtypes.bfloat16).astype(np.float64), axis, -1)
    blocks = v.reshape(v.shape[:-1] + (-1, 32))
    amax = np.abs(blocks).max(-1, keepdims=True)
    byte = np.maximum(np.where(amax > 0, np.frexp(amax)[1] - 1 + 127, 0) - down, 1)
    scale = np.exp2(byte - 127.0)
    codes = (blocks / scale).astype(np.float32).astype(dtype).astype(np.float64)
    return np.moveaxis((codes * scale).reshape(v.shape), -1, axis)


WIDE = False


def mx_kscale(k):
    if not WIDE:
        return np.ones(k)
    levels = np.array([10, -10, 5, -5, 0])
    if k % 512:
        return np.exp2(np.random.permutation(np.resize(levels, k // 32))).repeat(32)
    a = np.empty((k // 512, 16))
    for p in range(k // 512):
        a[p, :8] = np.random.permutation(np.resize(levels, 8))
        for g in range(8):
            far = levels[np.abs(levels - a[p, g]) >= 10]
            a[p, g + 8] = far[np.random.randint(len(far))]
    return np.exp2(a.ravel()).repeat(32)


def f64(x):
    return np.asarray(x).astype(np.float64)


def striped(idx):
    return np.tile(idx.reshape(-1, 16).T, (8, 1)).astype(np.uint16)


def unstriped(offs):
    return offs[:16].T.reshape(-1).astype(np.int64)


def striped8(idx):
    return np.concatenate([x.reshape(-1, 16).T for x in idx]).astype(np.uint16)


def runs(offs, k):
    lists = np.stack([offs[16 * r : 16 * r + 16].T.reshape(-1) for r in range(8)]).astype(np.int64)
    return lists[np.arange(k) % 512 // 64]


def pack_weight(w):
    k, n = w.shape
    w = f64(np.asarray(w, np.float32).astype(ml_dtypes.bfloat16)).reshape(k // 32, 32, n)
    amax = np.abs(w).max(1)
    byte = np.clip(np.where(amax > 0, np.frexp(amax)[1] - 1 + 127 - 7, 1), 1, 254)
    scaled = (w * np.exp2(127.0 - byte)[:, None, :]).reshape(k, n).astype(np.float32)
    words = np.ascontiguousarray(scaled.reshape(k // 512, 128, 4, n).transpose(0, 1, 3, 2)).astype(ml_dtypes.float8_e4m3fn).view(np.uint8)
    return words, np.ascontiguousarray(byte.astype(np.uint8).reshape(k // 512, 16, n))


def unpack_weight(words, scales):
    g, p, n, _ = words.shape
    vals = np.ascontiguousarray(words).view(ml_dtypes.float8_e4m3fn).astype(np.float64) * np.repeat(np.exp2(scales.astype(np.float64) - 127.0), 8, axis=1)[..., None]
    return vals.transpose(0, 1, 3, 2).reshape(g * 512, n)


def sigmoid(v):
    return 1.0 / (1.0 + np.exp(-np.maximum(v, -700.0)))


K, T, S, N, H = 512, 2048, 256, 512, 512


def setup_inputs():
    n = np.random.standard_normal
    s = mx_kscale(K)[:, None]
    u = mx_kscale(H)
    packed_xT = pack_weight(n((K, T)) * s)
    return {
        "x_words": packed_xT[0],
        "x_scales": packed_xT[1],
        "w1": (n((K, H)) / np.sqrt(K) / s).astype(np.float32),
        "gn": (np.random.uniform(0.5, 1.5, (H, 1)) * u[:, None]).astype(np.float32),
        "gm": (np.random.uniform(0.5, 1.5, (H, 1)) * u[:, None]).astype(np.float32),
        "w2": (n((H, N)) / np.sqrt(2 * H) / u[:, None]).astype(np.float32),
        "w3": (n((H, N)) / np.sqrt(2 * H) / u[:, None]).astype(np.float32),
        "offs": striped(np.random.permutation(T)[:S]),
        "n1": striped8(np.stack([np.random.permutation(S) for _ in range(8)])),
        "n2": striped8(np.stack([np.random.permutation(S) for _ in range(8)])),
        "n3": striped(np.random.permutation(S)),
        "n4": striped(np.random.permutation(S)),
        "n5": striped8(np.stack([np.random.permutation(S) for _ in range(8)])),
        "n6": striped8(np.stack([np.random.permutation(S) for _ in range(8)])),
    }


def reference(x_words, x_scales, w1, gn, gm, w2, w3, offs, n1, n2, n3, n4, n5, n6):
    xq = unpack_weight(x_words, x_scales)[:, unstriped(offs)]
    y = mxq(f64(w1), 0, "e4m3").T @ xq
    pa = y[np.arange(H)[:, None], runs(n1, H)]
    pb = y[np.arange(H)[:, None], runs(n2, H)]
    z = f64(gn) * (np.maximum(np.maximum(y, pa), pb) - (0.5 * (np.minimum(np.minimum(y, pa), pb))))
    st = y * (sigmoid(y[:, unstriped(n3)]))
    z2 = f64(gm) * (st - st[:, unstriped(n4)])
    h = mxq(f64(w2), 0, "e4m3").T @ mxq(z, 0, "e4m3") + mxq(f64(w3), 0, "e4m3").T @ mxq(z2, 0, "e4m3")
    return 0.75 * (h[np.arange(N)[:, None], runs(n5, N)] + h[np.arange(N)[:, None], runs(n6, N)]) - h

@@ -1,0 +1,203 @@
+from contextlib import ExitStack
+
+import concourse.mybir as mybir
+
+K, T, S, H, N = 512, 2048, 256, 512, 512
+FLOPS = 2 * S * (K * H + 2 * H * N)
+
+F32 = mybir.dt.float32
+BF16 = mybir.dt.bfloat16
+I32 = mybir.dt.int32
+U32 = mybir.dt.uint32
+U16 = mybir.dt.uint16
+U8 = mybir.dt.uint8
+FP8X4 = mybir.dt.float8_e4m3fn_x4
+ALU = mybir.AluOpType
+ACT = mybir.ActivationFunctionType
+
+P = 128
+PACK = 4
+WINDOW = 2 * S
+RUN = 4
+
+
+def tile_picked_joinrangehopglap_none_p_kernel(tc, x_words, x_scales, w1, gn, gm, w2, w3, offs, n1, n2, n3, n4, n5, n6, out):
+    nc = tc.nc
+    with ExitStack() as ctx:
+        keep = ctx.enter_context(tc.tile_pool(name="keep", bufs=1))
+        psum = ctx.enter_context(tc.psum_pool(name="psum", bufs=1))
+
+        def load_list(name, src):
+            offsets = keep.tile([P, S // 16], U16, name=name)
+            nc.sync.dma_start(offsets[:], src)
+            return offsets
+
+        def load_weight(name, src):
+            raw = keep.tile([P, PACK, H], F32, name=name)
+            nc.sync.dma_start(raw[:], src.rearrange("(p j) c -> p j c", j=PACK))
+            return raw
+
+        def round_half(engine_copy, name, raw, half):
+            rounded = keep.tile([P, 2, P, PACK], BF16, name=name, align_bytes=64)
+            src = raw[:].rearrange("p j (m t) -> p m j t", t=PACK)[:, :, :, 2 * half : 2 * half + 2]
+            engine_copy(rounded[:].rearrange("p t m j -> p m j t"), src)
+            return rounded
+
+        def quantize(name, values, words):
+            codes = keep.tile([P, words], U32, name=name + "_codes", align_bytes=64)
+            scales = keep.tile([P, words], U8, name=name + "_scales", align_bytes=64)
+            nc.vector.quantize_mx(out=codes[:].bitcast(FP8X4), scales=scales[:], in_=values)
+            return codes, scales
+
+        def quantize_half(name, rounded):
+            return quantize(name, rounded[:].rearrange("p t m j -> p (t m j)"), 2 * P)
+
+        def multiply(acc, weight_halves, t, moving, start, stop):
+            codes, scales = weight_halves[t // 2]
+            cols = slice((t % 2) * P, (t % 2 + 1) * P)
+            nc.tensor.matmul_mx(
+                out=acc,
+                lhsT=codes[:, cols].bitcast(FP8X4),
+                lhsT_scale=scales[:, cols],
+                rhs=moving[0][:].bitcast(FP8X4),
+                rhs_scale=moving[1][:],
+                start=start,
+                stop=stop,
+            )
+
+        scale_table = keep.tile([P, T], U8, name="scale_table")
+        nc.vector.memset(scale_table[:].bitcast(I32), 0)
+        offs_t = load_list("offs_t", offs)
+        w1_raw = load_weight("w1_raw", w1)
+        word_table = keep.tile([P, T], I32, name="word_table")
+        nc.sync.dma_start(word_table[:], x_words[0].rearrange("p c r -> p (c r)").bitcast(I32))
+        for q in range(4):
+            queue = nc.scalar if q < 2 else nc.gpsimd
+            queue.dma_start(scale_table[32 * q : 32 * q + 4, :].bitcast(I32), x_scales[0, 4 * q : 4 * q + 4, :].bitcast(I32))
+        gn_t = keep.tile([P, PACK], F32, name="gn_t")
+        gm_t = keep.tile([P, PACK], F32, name="gm_t")
+        n3_t = load_list("n3_t", n3)
+        n1_t = load_list("n1_t", n1)
+        nc.sync.dma_start(gm_t[:], gm.rearrange("(p t) o -> p (t o)", t=PACK))
+        n2_t = load_list("n2_t", n2)
+        w2_raw = load_weight("w2_raw", w2)
+        w3_raw = load_weight("w3_raw", w3)
+        n4_t = load_list("n4_t", n4)
+        nc.sync.dma_start(gn_t[:], gn.rearrange("(p t) o -> p (t o)", t=PACK))
+        n5_t = load_list("n5_t", n5)
+        n6_t = load_list("n6_t", n6)
+
+        y_win = [keep.tile([P, WINDOW], F32, name=f"y_win{t}") for t in range(PACK)]
+        h_win = [keep.tile([P, WINDOW], F32, name=f"h_win{t}") for t in range(PACK)]
+        for win in y_win + h_win:
+            nc.vector.memset(win[:, S:], 0.0)
+
+        w1_b = round_half(nc.scalar.copy, "w1_r1", w1_raw, 1)
+        w1_a = round_half(nc.vector.tensor_copy, "w1_r0", w1_raw, 0)
+        w1_q = [quantize_half("w1_q0", w1_a)]
+        x_scale = keep.tile([P, S], U8, name="x_scale", align_bytes=64)
+        nc.vector.tensor_copy(x_scale[:], scale_table[:].indirect(offs_t[:]))
+        w1_q.append(quantize_half("w1_q1", w1_b))
+        x_code = keep.tile([P, S], U32, name="x_code", align_bytes=64)
+        nc.vector.tensor_copy(x_code[:], word_table[:].bitcast(U32).indirect(offs_t[:]))
+
+        y_ps = [psum.tile([P, 2, S], F32, name=f"y_ps{q}") for q in range(2)]
+        for t in range(PACK):
+            multiply(y_ps[t // 2][:, t % 2, :], w1_q, t, (x_code, x_scale), True, True)
+        for t in range(PACK):
+            nc.vector.tensor_copy(y_win[t][:, :S], y_ps[t // 2][:, t % 2, :])
+
+        st_win = keep.tile([P, PACK, WINDOW], F32, name="st_win")
+        pa = keep.tile([P, PACK, S], F32, name="pa")
+        pb = keep.tile([P, PACK, S], F32, name="pb")
+        hi1 = keep.tile([P, PACK, S], F32, name="hi1")
+        lo1 = keep.tile([P, PACK, S], F32, name="lo1")
+        hi2 = keep.tile([P, PACK, S], F32, name="hi2")
+        lo2 = keep.tile([P, PACK, S], F32, name="lo2")
+        span = keep.tile([P, PACK, S], F32, name="span")
+        st_n4 = keep.tile([P, PACK, S], F32, name="st_n4")
+
+        def y_plane(t):
+            return y_ps[t // 2][:, t % 2, :]
+
+        def fetch(dst, win, offsets, func=ACT.Copy):
+            nc.scalar.activation(dst, win.indirect(offsets[:]), func)
+
+        def gate(t):
+            nc.vector.scalar_tensor_tensor(st_win[:, t, :S], y_plane(t), gm_t[:, t : t + 1], st_win[:, t, S:], ALU.mult, ALU.mult)
+
+        def extremes(q):
+            pair = slice(2 * q, 2 * q + 2)
+            nc.vector.tensor_tensor(hi1[:, pair, :], pa[:, pair, :], y_ps[q][:], ALU.max)
+            nc.vector.tensor_tensor(lo1[:, pair, :], pa[:, pair, :], y_ps[q][:], ALU.min)
+            nc.vector.tensor_tensor(hi2[:, pair, :], hi1[:, pair, :], pb[:, pair, :], ALU.max)
+            nc.vector.tensor_tensor(lo2[:, pair, :], lo1[:, pair, :], pb[:, pair, :], ALU.min)
+
+        def spread(q):
+            pair = slice(2 * q, 2 * q + 2)
+            nc.vector.scalar_tensor_tensor(span[:, pair, :], lo2[:, pair, :], -0.5, hi2[:, pair, :], ALU.mult, ALU.add)
+
+        def neighbours(q):
+            for dst, offsets in ((pa, n1_t), (pb, n2_t)):
+                for t in (2 * q, 2 * q + 1):
+                    fetch(dst[:, t, :], y_win[t][:], offsets)
+
+        def by_runs(planes):
+            return planes.rearrange("p t (c i) -> p c t i", i=RUN)
+
+        def interleaved(tile):
+            return tile[:].rearrange("p (c i) t -> p c t i", i=RUN)
+
+        fetch(st_win[:, 0, S:], y_win[0][:], n3_t, ACT.Sigmoid)
+        neighbours(0)
+        fetch(st_win[:, 1, S:], y_win[1][:], n3_t, ACT.Sigmoid)
+        neighbours(1)
+        fetch(st_win[:, 2, S:], y_win[2][:], n3_t, ACT.Sigmoid)
+        fetch(st_win[:, 3, S:], y_win[3][:], n3_t, ACT.Sigmoid)
+
+        w2_r = [round_half(nc.vector.tensor_copy, f"w2_r{u}", w2_raw, u) for u in range(2)]
+        w2_q = [quantize_half(f"w2_q{u}", w2_r[u]) for u in range(2)]
+        gate(0)
+        extremes(0)
+        gate(1)
+        spread(0)
+        extremes(1)
+        gate(2)
+        gate(3)
+        spread(1)
+
+        w3_r = []
+        for u in range(2):
+            for t in (2 * u, 2 * u + 1):
+                fetch(st_n4[:, t, :], st_win[:, t, :], n4_t)
+            w3_r.append(round_half(nc.scalar.copy, f"w3_r{u}", w3_raw, u))
+
+        z = keep.tile([P, S, PACK], BF16, name="z", align_bytes=64)
+        gn_wide = gn_t[:].unsqueeze(1).unsqueeze(3).to_broadcast([P, S // RUN, PACK, RUN])
+        nc.vector.tensor_tensor(interleaved(z), by_runs(span[:]), gn_wide, ALU.mult)
+        w3_q = [quantize_half("w3_q0", w3_r[0])]
+        z_q = quantize("z_q", z[:].rearrange("p c t -> p (c t)"), S)
+        h_ps = [psum.tile([P, S], F32, name=f"h_ps{t}") for t in range(PACK)]
+        for t in range(PACK):
+            multiply(h_ps[t][:], w2_q, t, z_q, True, False)
+
+        z2 = keep.tile([P, S, PACK], BF16, name="z2", align_bytes=64)
+        nc.vector.tensor_tensor(interleaved(z2), by_runs(st_win[:, :, :S]), by_runs(st_n4[:]), ALU.subtract)
+        w3_q.append(quantize_half("w3_q1", w3_r[1]))
+        z2_q = quantize("z2_q", z2[:].rearrange("p c t -> p (c t)"), S)
+        for t in range(PACK):
+            multiply(h_ps[t][:], w3_q, t, z2_q, False, True)
+
+        out_rows = out.rearrange("(p t) j -> p t j", t=PACK)
+        for t in range(PACK):
+            nc.vector.tensor_copy(h_win[t][:, :S], h_ps[t][:])
+        for t in range(PACK):
+            h_n5 = keep.tile([P, S], F32, name=f"h_n5_{t}")
+            h_n6 = keep.tile([P, S], F32, name=f"h_n6_{t}")
+            part = keep.tile([P, S], F32, name=f"part{t}")
+            result = keep.tile([P, S], F32, name=f"result{t}")
+            nc.scalar.activation(h_n5[:], h_win[t][:].indirect(n5_t[:]), ACT.Copy)
+            nc.vector.scalar_tensor_tensor(part[:], h_n5[:], 0.75, h_ps[t][:], ALU.mult, ALU.subtract)
+            nc.scalar.activation(h_n6[:], h_win[t][:].indirect(n6_t[:]), ACT.Copy)
+            nc.vector.scalar_tensor_tensor(result[:], h_n6[:], 0.75, part[:], ALU.mult, ALU.add)
+            nc.sync.dma_start(out_rows[:, t, :], result[:])

@@ -19,6 +19,7 @@ P = 128
 PACK = 4
 WINDOW = 2 * S
 RUN = 4
+HALF = 2 * P * PACK
 
 
 def tile_picked_joinrangehopglap_none_p_kernel(tc, x_words, x_scales, w1, gn, gm, w2, w3, offs, n1, n2, n3, n4, n5, n6, out):
@@ -37,11 +38,13 @@ def tile_picked_joinrangehopglap_none_p_kernel(tc, x_words, x_scales, w1, gn, gm
             nc.sync.dma_start(raw[:], src.rearrange("(p j) c -> p j c", j=PACK))
             return raw
 
-        def round_half(engine_copy, name, raw, half):
-            rounded = keep.tile([P, 2, P, PACK], BF16, name=name, align_bytes=64)
+        def round_half(engine_copy, rounded, raw, half):
             src = raw[:].rearrange("p j (m t) -> p m j t", t=PACK)[:, :, :, 2 * half : 2 * half + 2]
-            engine_copy(rounded[:].rearrange("p t m j -> p m j t"), src)
+            engine_copy(rounded.rearrange("p (t m j) -> p m j t", t=2, j=PACK), src)
             return rounded
+
+        def half_tile(name):
+            return keep.tile([P, HALF], BF16, name=name, align_bytes=64)[:]
 
         def quantize(name, values, words):
             codes = keep.tile([P, words], U32, name=name + "_codes", align_bytes=64)
@@ -50,7 +53,7 @@ def tile_picked_joinrangehopglap_none_p_kernel(tc, x_words, x_scales, w1, gn, gm
             return codes, scales
 
         def quantize_half(name, rounded):
-            return quantize(name, rounded[:].rearrange("p t m j -> p (t m j)"), 2 * P)
+            return quantize(name, rounded, 2 * P)
 
         def multiply(acc, weight_halves, t, moving, start, stop):
             codes, scales = weight_halves[t // 2]
@@ -67,20 +70,19 @@ def tile_picked_joinrangehopglap_none_p_kernel(tc, x_words, x_scales, w1, gn, gm
 
         scale_table = keep.tile([P, T], U8, name="scale_table")
         nc.vector.memset(scale_table[:].bitcast(I32), 0)
-        offs_t = load_list("offs_t", offs)
-        w1_raw = load_weight("w1_raw", w1)
-        word_table = keep.tile([P, T], I32, name="word_table")
-        nc.sync.dma_start(word_table[:], x_words[0].rearrange("p c r -> p (c r)").bitcast(I32))
-        for q in range(4):
-            queue = nc.scalar if q < 2 else nc.gpsimd
-            queue.dma_start(scale_table[32 * q : 32 * q + 4, :].bitcast(I32), x_scales[0, 4 * q : 4 * q + 4, :].bitcast(I32))
         gn_t = keep.tile([P, PACK], F32, name="gn_t")
         gm_t = keep.tile([P, PACK], F32, name="gm_t")
+        for q in range(4):
+            nc.sync.dma_start(scale_table[32 * q : 32 * q + 4, :].bitcast(I32), x_scales[0, 4 * q : 4 * q + 4, :].bitcast(I32))
+        offs_t = load_list("offs_t", offs)
+        w1_raw = load_weight("w1_raw", w1)
         n3_t = load_list("n3_t", n3)
+        word_table = keep.tile([P, T], I32, name="word_table")
+        nc.sync.dma_start(word_table[:], x_words[0].rearrange("p c r -> p (c r)").bitcast(I32))
         n1_t = load_list("n1_t", n1)
+        w2_raw = load_weight("w2_raw", w2)
         nc.sync.dma_start(gm_t[:], gm.rearrange("(p t) o -> p (t o)", t=PACK))
         n2_t = load_list("n2_t", n2)
-        w2_raw = load_weight("w2_raw", w2)
         w3_raw = load_weight("w3_raw", w3)
         n4_t = load_list("n4_t", n4)
         nc.sync.dma_start(gn_t[:], gn.rearrange("(p t) o -> p (t o)", t=PACK))
@@ -92,8 +94,8 @@ def tile_picked_joinrangehopglap_none_p_kernel(tc, x_words, x_scales, w1, gn, gm
         for win in y_win + h_win:
             nc.vector.memset(win[:, S:], 0.0)
 
-        w1_b = round_half(nc.scalar.copy, "w1_r1", w1_raw, 1)
-        w1_a = round_half(nc.vector.tensor_copy, "w1_r0", w1_raw, 0)
+        w1_b = round_half(nc.scalar.copy, half_tile("w1_r1"), w1_raw, 1)
+        w1_a = round_half(nc.vector.tensor_copy, half_tile("w1_r0"), w1_raw, 0)
         w1_q = [quantize_half("w1_q0", w1_a)]
         x_scale = keep.tile([P, S], U8, name="x_scale", align_bytes=64)
         nc.vector.tensor_copy(x_scale[:], scale_table[:].indirect(offs_t[:]))
@@ -114,8 +116,8 @@ def tile_picked_joinrangehopglap_none_p_kernel(tc, x_words, x_scales, w1, gn, gm
         lo1 = keep.tile([P, PACK, S], F32, name="lo1")
         hi2 = keep.tile([P, PACK, S], F32, name="hi2")
         lo2 = keep.tile([P, PACK, S], F32, name="lo2")
-        span = keep.tile([P, PACK, S], F32, name="span")
-        st_n4 = keep.tile([P, PACK, S], F32, name="st_n4")
+        span = keep.tile([P, PACK, S], F32, name="span", tag="span", align_bytes=64)
+        st_n4 = keep.tile([P, PACK, S], F32, name="st_n4", tag="st_n4", align_bytes=64)
 
         def y_plane(t):
             return y_ps[t // 2][:, t % 2, :]
@@ -150,47 +152,52 @@ def tile_picked_joinrangehopglap_none_p_kernel(tc, x_words, x_scales, w1, gn, gm
 
         fetch(st_win[:, 0, S:], y_win[0][:], n3_t, ACT.Sigmoid)
         neighbours(0)
-        fetch(st_win[:, 1, S:], y_win[1][:], n3_t, ACT.Sigmoid)
         neighbours(1)
-        fetch(st_win[:, 2, S:], y_win[2][:], n3_t, ACT.Sigmoid)
-        fetch(st_win[:, 3, S:], y_win[3][:], n3_t, ACT.Sigmoid)
+        for t in range(1, PACK):
+            fetch(st_win[:, t, S:], y_win[t][:], n3_t, ACT.Sigmoid)
 
-        w2_r = [round_half(nc.vector.tensor_copy, f"w2_r{u}", w2_raw, u) for u in range(2)]
-        w2_q = [quantize_half(f"w2_q{u}", w2_r[u]) for u in range(2)]
+        w2_r = [round_half(nc.vector.tensor_copy, half_tile("w2_r0"), w2_raw, 0)]
         gate(0)
+        w2_q = [quantize_half("w2_q0", w2_r[0])]
+        nc.vector.tensor_copy(st_n4[:, 0, :], st_win[:, 0, :].indirect(n4_t[:]))
         extremes(0)
-        gate(1)
         spread(0)
         extremes(1)
+        gate(1)
+        spread(1)
         gate(2)
         gate(3)
-        spread(1)
-
-        w3_r = []
-        for u in range(2):
-            for t in (2 * u, 2 * u + 1):
-                fetch(st_n4[:, t, :], st_win[:, t, :], n4_t)
-            w3_r.append(round_half(nc.scalar.copy, f"w3_r{u}", w3_raw, u))
+        for t in range(1, PACK):
+            fetch(st_n4[:, t, :], st_win[:, t, :], n4_t)
 
         z = keep.tile([P, S, PACK], BF16, name="z", align_bytes=64)
         gn_wide = gn_t[:].unsqueeze(1).unsqueeze(3).to_broadcast([P, S // RUN, PACK, RUN])
         nc.vector.tensor_tensor(interleaved(z), by_runs(span[:]), gn_wide, ALU.mult)
-        w3_q = [quantize_half("w3_q0", w3_r[0])]
+        w3_rounded = keep.tile([P, 2 * HALF], BF16, name="w3_rounded", tag="span", align_bytes=64)
+        w3_r = [round_half(nc.scalar.copy, w3_rounded[:, u * HALF : (u + 1) * HALF], w3_raw, u) for u in range(2)]
         z_q = quantize("z_q", z[:].rearrange("p c t -> p (c t)"), S)
         h_ps = [psum.tile([P, S], F32, name=f"h_ps{t}") for t in range(PACK)]
-        for t in range(PACK):
+        for t in range(2):
             multiply(h_ps[t][:], w2_q, t, z_q, True, False)
 
         z2 = keep.tile([P, S, PACK], BF16, name="z2", align_bytes=64)
         nc.vector.tensor_tensor(interleaved(z2), by_runs(st_win[:, :, :S]), by_runs(st_n4[:]), ALU.subtract)
-        w3_q.append(quantize_half("w3_q1", w3_r[1]))
+        w3_q = [quantize_half("w3_q0", w3_r[0])]
         z2_q = quantize("z2_q", z2[:].rearrange("p c t -> p (c t)"), S)
-        for t in range(PACK):
+        for t in range(2):
             multiply(h_ps[t][:], w3_q, t, z2_q, False, True)
+        nc.scalar.copy(h_win[0][:, :S], h_ps[0][:])
+        w2_late = keep.tile([P, HALF], BF16, name="w2_late", tag="st_n4", align_bytes=64)
+        w2_r.append(round_half(nc.vector.tensor_copy, w2_late[:], w2_raw, 1))
+        nc.vector.tensor_copy(h_win[1][:, :S], h_ps[1][:])
+        w2_q.append(quantize_half("w2_q1", w2_r[1]))
+        w3_q.append(quantize_half("w3_q1", w3_r[1]))
+        for t in range(2, PACK):
+            multiply(h_ps[t][:], w2_q, t, z_q, True, False)
+            multiply(h_ps[t][:], w3_q, t, z2_q, False, True)
+            nc.vector.tensor_copy(h_win[t][:, :S], h_ps[t][:])
 
         out_rows = out.rearrange("(p t) j -> p t j", t=PACK)
-        for t in range(PACK):
-            nc.vector.tensor_copy(h_win[t][:, :S], h_ps[t][:])
         for t in range(PACK):
             h_n5 = keep.tile([P, S], F32, name=f"h_n5_{t}")
             h_n6 = keep.tile([P, S], F32, name=f"h_n6_{t}")
@@ -198,6 +205,10 @@ def tile_picked_joinrangehopglap_none_p_kernel(tc, x_words, x_scales, w1, gn, gm
             result = keep.tile([P, S], F32, name=f"result{t}")
             nc.scalar.activation(h_n5[:], h_win[t][:].indirect(n5_t[:]), ACT.Copy)
             nc.vector.scalar_tensor_tensor(part[:], h_n5[:], 0.75, h_ps[t][:], ALU.mult, ALU.subtract)
-            nc.scalar.activation(h_n6[:], h_win[t][:].indirect(n6_t[:]), ACT.Copy)
-            nc.vector.scalar_tensor_tensor(result[:], h_n6[:], 0.75, part[:], ALU.mult, ALU.add)
-            nc.sync.dma_start(out_rows[:, t, :], result[:])
+            pieces = 2 if t == PACK - 1 else 1
+            for u in range(pieces):
+                cols = slice(u * S // pieces, (u + 1) * S // pieces)
+                entries = n6_t[:, u * 16 // pieces : (u + 1) * 16 // pieces]
+                nc.scalar.activation(h_n6[:, cols], h_win[t][:].indirect(entries), ACT.Copy)
+                nc.vector.scalar_tensor_tensor(result[:, cols], h_n6[:, cols], 0.75, part[:, cols], ALU.mult, ALU.add)
+                nc.sync.dma_start(out_rows[:, t, cols], result[:, cols])

@@ -74,15 +74,15 @@ def tile_picked_joinrangehopglap_none_p_kernel(tc, x_words, x_scales, w1, gn, gm
         gm_t = keep.tile([P, PACK], F32, name="gm_t")
         for q in range(4):
             nc.sync.dma_start(scale_table[32 * q : 32 * q + 4, :].bitcast(I32), x_scales[0, 4 * q : 4 * q + 4, :].bitcast(I32))
-        offs_t = load_list("offs_t", offs)
         w1_raw = load_weight("w1_raw", w1)
+        offs_t = load_list("offs_t", offs)
         n3_t = load_list("n3_t", n3)
         word_table = keep.tile([P, T], I32, name="word_table")
         nc.sync.dma_start(word_table[:], x_words[0].rearrange("p c r -> p (c r)").bitcast(I32))
         n1_t = load_list("n1_t", n1)
-        w2_raw = load_weight("w2_raw", w2)
         nc.sync.dma_start(gm_t[:], gm.rearrange("(p t) o -> p (t o)", t=PACK))
         n2_t = load_list("n2_t", n2)
+        w2_raw = load_weight("w2_raw", w2)
         w3_raw = load_weight("w3_raw", w3)
         n4_t = load_list("n4_t", n4)
         nc.sync.dma_start(gn_t[:], gn.rearrange("(p t) o -> p (t o)", t=PACK))
@@ -117,7 +117,7 @@ def tile_picked_joinrangehopglap_none_p_kernel(tc, x_words, x_scales, w1, gn, gm
         hi2 = keep.tile([P, PACK, S], F32, name="hi2")
         lo2 = keep.tile([P, PACK, S], F32, name="lo2")
         span = keep.tile([P, PACK, S], F32, name="span", tag="span", align_bytes=64)
-        st_n4 = keep.tile([P, PACK, S], F32, name="st_n4", tag="st_n4", align_bytes=64)
+        st_n4 = keep.tile([P, PACK, S], F32, name="st_n4")
 
         def y_plane(t):
             return y_ps[t // 2][:, t % 2, :]
@@ -148,7 +148,7 @@ def tile_picked_joinrangehopglap_none_p_kernel(tc, x_words, x_scales, w1, gn, gm
             return planes.rearrange("p t (c i) -> p c t i", i=RUN)
 
         def interleaved(tile):
-            return tile[:].rearrange("p (c i) t -> p c t i", i=RUN)
+            return tile.rearrange("p (c i t) -> p c t i", i=RUN, t=PACK)
 
         fetch(st_win[:, 0, S:], y_win[0][:], n3_t, ACT.Sigmoid)
         neighbours(0)
@@ -159,35 +159,48 @@ def tile_picked_joinrangehopglap_none_p_kernel(tc, x_words, x_scales, w1, gn, gm
         w2_r = [round_half(nc.vector.tensor_copy, half_tile("w2_r0"), w2_raw, 0)]
         gate(0)
         w2_q = [quantize_half("w2_q0", w2_r[0])]
-        nc.vector.tensor_copy(st_n4[:, 0, :], st_win[:, 0, :].indirect(n4_t[:]))
         extremes(0)
         spread(0)
         extremes(1)
         gate(1)
-        spread(1)
         gate(2)
+        spread(1)
         gate(3)
-        for t in range(1, PACK):
+        for t in range(PACK - 1):
             fetch(st_n4[:, t, :], st_win[:, t, :], n4_t)
+        halves = [slice(0, S // 2), slice(S // 2, S)]
+        for u, cols in enumerate(halves):
+            nc.scalar.activation(st_n4[:, PACK - 1, cols], st_win[:, PACK - 1, :].indirect(n4_t[:, 8 * u : 8 * u + 8]), ACT.Copy)
 
-        z = keep.tile([P, S, PACK], BF16, name="z", align_bytes=64)
+        z = keep.tile([P, S * PACK], BF16, name="z", align_bytes=64)
         gn_wide = gn_t[:].unsqueeze(1).unsqueeze(3).to_broadcast([P, S // RUN, PACK, RUN])
-        nc.vector.tensor_tensor(interleaved(z), by_runs(span[:]), gn_wide, ALU.mult)
+        nc.vector.tensor_tensor(interleaved(z[:]), by_runs(span[:]), gn_wide, ALU.mult)
         w3_rounded = keep.tile([P, 2 * HALF], BF16, name="w3_rounded", tag="span", align_bytes=64)
         w3_r = [round_half(nc.scalar.copy, w3_rounded[:, u * HALF : (u + 1) * HALF], w3_raw, u) for u in range(2)]
-        z_q = quantize("z_q", z[:].rearrange("p c t -> p (c t)"), S)
+        z_q = quantize("z_q", z[:], S)
         h_ps = [psum.tile([P, S], F32, name=f"h_ps{t}") for t in range(PACK)]
         for t in range(2):
             multiply(h_ps[t][:], w2_q, t, z_q, True, False)
 
-        z2 = keep.tile([P, S, PACK], BF16, name="z2", align_bytes=64)
-        nc.vector.tensor_tensor(interleaved(z2), by_runs(st_win[:, :, :S]), by_runs(st_n4[:]), ALU.subtract)
+        z2 = keep.tile([P, S * PACK], BF16, name="z2", tag="z2", align_bytes=64)
+        z2_codes = keep.tile([P, S], U32, name="z2_codes", align_bytes=64)
+        z2_scales = keep.tile([P, S], U8, name="z2_scales", align_bytes=64)
+        z2_q = (z2_codes, z2_scales)
+        for cols in halves:
+            nc.vector.tensor_tensor(interleaved(z2[:, cols.start * PACK : cols.stop * PACK]), by_runs(st_win[:, :, cols]), by_runs(st_n4[:, :, cols]), ALU.subtract)
+
+        def quantize_z2(cols):
+            values = z2[:, cols.start * PACK : cols.stop * PACK]
+            nc.vector.quantize_mx(out=z2_codes[:, cols].bitcast(FP8X4), scales=z2_scales[:, cols], in_=values)
+
+        quantize_z2(halves[0])
         w3_q = [quantize_half("w3_q0", w3_r[0])]
-        z2_q = quantize("z2_q", z2[:].rearrange("p c t -> p (c t)"), S)
+        quantize_z2(halves[1])
         for t in range(2):
-            multiply(h_ps[t][:], w3_q, t, z2_q, False, True)
+            for u, cols in enumerate(halves):
+                multiply(h_ps[t][:, cols], w3_q, t, (z2_codes[:, cols], z2_scales[:, cols]), False, u == 1)
         nc.scalar.copy(h_win[0][:, :S], h_ps[0][:])
-        w2_late = keep.tile([P, HALF], BF16, name="w2_late", tag="st_n4", align_bytes=64)
+        w2_late = keep.tile([P, HALF], BF16, name="w2_late", tag="z2", align_bytes=64)
         w2_r.append(round_half(nc.vector.tensor_copy, w2_late[:], w2_raw, 1))
         nc.vector.tensor_copy(h_win[1][:, :S], h_ps[1][:])
         w2_q.append(quantize_half("w2_q1", w2_r[1]))

from contextlib import ExitStack

import concourse.mybir as mybir

K, T, S, H, N = 512, 2048, 256, 512, 512
FLOPS = 2 * S * (K * H + 2 * H * N)

F32 = mybir.dt.float32
BF16 = mybir.dt.bfloat16
I32 = mybir.dt.int32
U32 = mybir.dt.uint32
U16 = mybir.dt.uint16
U8 = mybir.dt.uint8
FP8X4 = mybir.dt.float8_e4m3fn_x4
ALU = mybir.AluOpType
ACT = mybir.ActivationFunctionType

P = 128
PACK = 4
WINDOW = 2 * S
RUN = 4
HALF = 2 * P * PACK


def tile_picked_joinrangehopglap_none_p_kernel(tc, x_words, x_scales, w1, gn, gm, w2, w3, offs, n1, n2, n3, n4, n5, n6, out):
    nc = tc.nc
    with ExitStack() as ctx:
        keep = ctx.enter_context(tc.tile_pool(name="keep", bufs=1))
        psum = ctx.enter_context(tc.psum_pool(name="psum", bufs=1))

        def load_list(name, src):
            offsets = keep.tile([P, S // 16], U16, name=name)
            nc.sync.dma_start(offsets[:], src)
            return offsets

        def load_weight(name, src):
            raw = keep.tile([P, PACK, H], F32, name=name)
            nc.sync.dma_start(raw[:], src.rearrange("(p j) c -> p j c", j=PACK))
            return raw

        def round_half(engine_copy, rounded, raw, half):
            src = raw[:].rearrange("p j (m t) -> p m j t", t=PACK)[:, :, :, 2 * half : 2 * half + 2]
            engine_copy(rounded.rearrange("p (t m j) -> p m j t", t=2, j=PACK), src)
            return rounded

        def half_tile(name):
            return keep.tile([P, HALF], BF16, name=name, align_bytes=64)[:]

        def quantize(name, values, words):
            codes = keep.tile([P, words], U32, name=name + "_codes", align_bytes=64)
            scales = keep.tile([P, words], U8, name=name + "_scales", align_bytes=64)
            nc.vector.quantize_mx(out=codes[:].bitcast(FP8X4), scales=scales[:], in_=values)
            return codes, scales

        def quantize_half(name, rounded):
            return quantize(name, rounded, 2 * P)

        def multiply(acc, weight_halves, t, moving, start, stop):
            codes, scales = weight_halves[t // 2]
            cols = slice((t % 2) * P, (t % 2 + 1) * P)
            nc.tensor.matmul_mx(
                out=acc,
                lhsT=codes[:, cols].bitcast(FP8X4),
                lhsT_scale=scales[:, cols],
                rhs=moving[0][:].bitcast(FP8X4),
                rhs_scale=moving[1][:],
                start=start,
                stop=stop,
            )

        scale_table = keep.tile([P, T], U8, name="scale_table")
        nc.vector.memset(scale_table[:].bitcast(I32), 0)
        gn_t = keep.tile([P, PACK], F32, name="gn_t")
        gm_t = keep.tile([P, PACK], F32, name="gm_t")
        for q in range(4):
            nc.sync.dma_start(scale_table[32 * q : 32 * q + 4, :].bitcast(I32), x_scales[0, 4 * q : 4 * q + 4, :].bitcast(I32))
        w1_raw = load_weight("w1_raw", w1)
        offs_t = load_list("offs_t", offs)
        n3_t = load_list("n3_t", n3)
        word_table = keep.tile([P, T], I32, name="word_table")
        nc.sync.dma_start(word_table[:], x_words[0].rearrange("p c r -> p (c r)").bitcast(I32))
        n1_t = load_list("n1_t", n1)
        nc.sync.dma_start(gm_t[:], gm.rearrange("(p t) o -> p (t o)", t=PACK))
        n2_t = load_list("n2_t", n2)
        w2_raw = load_weight("w2_raw", w2)
        w3_raw = load_weight("w3_raw", w3)
        n4_t = load_list("n4_t", n4)
        nc.sync.dma_start(gn_t[:], gn.rearrange("(p t) o -> p (t o)", t=PACK))
        n5_t = load_list("n5_t", n5)
        n6_t = load_list("n6_t", n6)

        y_win = [keep.tile([P, WINDOW], F32, name=f"y_win{t}") for t in range(PACK)]
        h_win = [keep.tile([P, WINDOW], F32, name=f"h_win{t}") for t in range(PACK)]
        for win in y_win + h_win:
            nc.vector.memset(win[:, S:], 0.0)

        w1_b = round_half(nc.scalar.copy, half_tile("w1_r1"), w1_raw, 1)
        w1_a = round_half(nc.vector.tensor_copy, half_tile("w1_r0"), w1_raw, 0)
        w1_q = [quantize_half("w1_q0", w1_a)]
        x_scale = keep.tile([P, S], U8, name="x_scale", align_bytes=64)
        nc.vector.tensor_copy(x_scale[:], scale_table[:].indirect(offs_t[:]))
        w1_q.append(quantize_half("w1_q1", w1_b))
        x_code = keep.tile([P, S], U32, name="x_code", align_bytes=64)
        nc.vector.tensor_copy(x_code[:], word_table[:].bitcast(U32).indirect(offs_t[:]))

        y_ps = [psum.tile([P, 2, S], F32, name=f"y_ps{q}") for q in range(2)]
        for t in range(PACK):
            multiply(y_ps[t // 2][:, t % 2, :], w1_q, t, (x_code, x_scale), True, True)
        for t in range(PACK):
            nc.vector.tensor_copy(y_win[t][:, :S], y_ps[t // 2][:, t % 2, :])

        st_win = keep.tile([P, PACK, WINDOW], F32, name="st_win")
        pa = keep.tile([P, PACK, S], F32, name="pa")
        pb = keep.tile([P, PACK, S], F32, name="pb")
        hi1 = keep.tile([P, PACK, S], F32, name="hi1")
        lo1 = keep.tile([P, PACK, S], F32, name="lo1")
        hi2 = keep.tile([P, PACK, S], F32, name="hi2")
        lo2 = keep.tile([P, PACK, S], F32, name="lo2")
        span = keep.tile([P, PACK, S], F32, name="span", tag="span", align_bytes=64)
        st_n4 = keep.tile([P, PACK, S], F32, name="st_n4")

        def y_plane(t):
            return y_ps[t // 2][:, t % 2, :]

        def fetch(dst, win, offsets, func=ACT.Copy):
            nc.scalar.activation(dst, win.indirect(offsets[:]), func)

        def gate(t):
            nc.vector.scalar_tensor_tensor(st_win[:, t, :S], y_plane(t), gm_t[:, t : t + 1], st_win[:, t, S:], ALU.mult, ALU.mult)

        def extremes(q):
            pair = slice(2 * q, 2 * q + 2)
            nc.vector.tensor_tensor(hi1[:, pair, :], pa[:, pair, :], y_ps[q][:], ALU.max)
            nc.vector.tensor_tensor(lo1[:, pair, :], pa[:, pair, :], y_ps[q][:], ALU.min)
            nc.vector.tensor_tensor(hi2[:, pair, :], hi1[:, pair, :], pb[:, pair, :], ALU.max)
            nc.vector.tensor_tensor(lo2[:, pair, :], lo1[:, pair, :], pb[:, pair, :], ALU.min)

        def spread(q):
            pair = slice(2 * q, 2 * q + 2)
            nc.vector.scalar_tensor_tensor(span[:, pair, :], lo2[:, pair, :], -0.5, hi2[:, pair, :], ALU.mult, ALU.add)

        def neighbours(q):
            for dst, offsets in ((pa, n1_t), (pb, n2_t)):
                for t in (2 * q, 2 * q + 1):
                    fetch(dst[:, t, :], y_win[t][:], offsets)

        def by_runs(planes):
            return planes.rearrange("p t (c i) -> p c t i", i=RUN)

        def interleaved(tile):
            return tile.rearrange("p (c i t) -> p c t i", i=RUN, t=PACK)

        fetch(st_win[:, 0, S:], y_win[0][:], n3_t, ACT.Sigmoid)
        neighbours(0)
        neighbours(1)
        for t in range(1, PACK):
            fetch(st_win[:, t, S:], y_win[t][:], n3_t, ACT.Sigmoid)

        w2_r = [round_half(nc.vector.tensor_copy, half_tile("w2_r0"), w2_raw, 0)]
        gate(0)
        w2_q = [quantize_half("w2_q0", w2_r[0])]
        extremes(0)
        spread(0)
        extremes(1)
        gate(1)
        gate(2)
        spread(1)
        gate(3)
        for t in range(PACK - 1):
            fetch(st_n4[:, t, :], st_win[:, t, :], n4_t)
        halves = [slice(0, S // 2), slice(S // 2, S)]
        for u, cols in enumerate(halves):
            nc.scalar.activation(st_n4[:, PACK - 1, cols], st_win[:, PACK - 1, :].indirect(n4_t[:, 8 * u : 8 * u + 8]), ACT.Copy)

        z = keep.tile([P, S * PACK], BF16, name="z", align_bytes=64)
        gn_wide = gn_t[:].unsqueeze(1).unsqueeze(3).to_broadcast([P, S // RUN, PACK, RUN])
        nc.vector.tensor_tensor(interleaved(z[:]), by_runs(span[:]), gn_wide, ALU.mult)
        w3_rounded = keep.tile([P, 2 * HALF], BF16, name="w3_rounded", tag="span", align_bytes=64)
        w3_r = [round_half(nc.scalar.copy, w3_rounded[:, u * HALF : (u + 1) * HALF], w3_raw, u) for u in range(2)]
        z_q = quantize("z_q", z[:], S)
        h_ps = [psum.tile([P, S], F32, name=f"h_ps{t}") for t in range(PACK)]
        for t in range(2):
            multiply(h_ps[t][:], w2_q, t, z_q, True, False)

        z2 = keep.tile([P, S * PACK], BF16, name="z2", tag="z2", align_bytes=64)
        z2_codes = keep.tile([P, S], U32, name="z2_codes", align_bytes=64)
        z2_scales = keep.tile([P, S], U8, name="z2_scales", align_bytes=64)
        z2_q = (z2_codes, z2_scales)
        for cols in halves:
            nc.vector.tensor_tensor(interleaved(z2[:, cols.start * PACK : cols.stop * PACK]), by_runs(st_win[:, :, cols]), by_runs(st_n4[:, :, cols]), ALU.subtract)

        def quantize_z2(cols):
            values = z2[:, cols.start * PACK : cols.stop * PACK]
            nc.vector.quantize_mx(out=z2_codes[:, cols].bitcast(FP8X4), scales=z2_scales[:, cols], in_=values)

        quantize_z2(halves[0])
        w3_q = [quantize_half("w3_q0", w3_r[0])]
        quantize_z2(halves[1])
        for t in range(2):
            for u, cols in enumerate(halves):
                multiply(h_ps[t][:, cols], w3_q, t, (z2_codes[:, cols], z2_scales[:, cols]), False, u == 1)
        nc.scalar.copy(h_win[0][:, :S], h_ps[0][:])
        w2_late = keep.tile([P, HALF], BF16, name="w2_late", tag="z2", align_bytes=64)
        w2_r.append(round_half(nc.vector.tensor_copy, w2_late[:], w2_raw, 1))
        nc.vector.tensor_copy(h_win[1][:, :S], h_ps[1][:])
        w2_q.append(quantize_half("w2_q1", w2_r[1]))
        w3_q.append(quantize_half("w3_q1", w3_r[1]))
        for t in range(2, PACK):
            multiply(h_ps[t][:], w2_q, t, z_q, True, False)
            multiply(h_ps[t][:], w3_q, t, z2_q, False, True)
            nc.vector.tensor_copy(h_win[t][:, :S], h_ps[t][:])

        out_rows = out.rearrange("(p t) j -> p t j", t=PACK)
        for t in range(PACK):
            h_n5 = keep.tile([P, S], F32, name=f"h_n5_{t}")
            h_n6 = keep.tile([P, S], F32, name=f"h_n6_{t}")
            part = keep.tile([P, S], F32, name=f"part{t}")
            result = keep.tile([P, S], F32, name=f"result{t}")
            nc.scalar.activation(h_n5[:], h_win[t][:].indirect(n5_t[:]), ACT.Copy)
            nc.vector.scalar_tensor_tensor(part[:], h_n5[:], 0.75, h_ps[t][:], ALU.mult, ALU.subtract)
            pieces = 2 if t == PACK - 1 else 1
            for u in range(pieces):
                cols = slice(u * S // pieces, (u + 1) * S // pieces)
                entries = n6_t[:, u * 16 // pieces : (u + 1) * 16 // pieces]
                nc.scalar.activation(h_n6[:, cols], h_win[t][:].indirect(entries), ACT.Copy)
                nc.vector.scalar_tensor_tensor(result[:, cols], h_n6[:, cols], 0.75, part[:, cols], ALU.mult, ALU.add)
                nc.sync.dma_start(out_rows[:, t, cols], result[:, cols])
